import numpy as np
import ml_dtypes


def mxq(x, axis, fmt="e4m3"):
    dtype, down = {"e4m3": (ml_dtypes.float8_e4m3fn, 7), "e5m2": (ml_dtypes.float8_e5m2, 14)}[fmt]
    v = np.moveaxis(np.asarray(x, np.float32).astype(ml_dtypes.bfloat16).astype(np.float64), axis, -1)
    blocks = v.reshape(v.shape[:-1] + (-1, 32))
    amax = np.abs(blocks).max(-1, keepdims=True)
    byte = np.maximum(np.where(amax > 0, np.frexp(amax)[1] - 1 + 127, 0) - down, 1)
    scale = np.exp2(byte - 127.0)
    codes = (blocks / scale).astype(np.float32).astype(dtype).astype(np.float64)
    return np.moveaxis((codes * scale).reshape(v.shape), -1, axis)


WIDE = False


def mx_kscale(k):
    if not WIDE:
        return np.ones(k)
    levels = np.array([10, -10, 5, -5, 0])
    if k % 512:
        return np.exp2(np.random.permutation(np.resize(levels, k // 32))).repeat(32)
    a = np.empty((k // 512, 16))
    for p in range(k // 512):
        a[p, :8] = np.random.permutation(np.resize(levels, 8))
        for g in range(8):
            far = levels[np.abs(levels - a[p, g]) >= 10]
            a[p, g + 8] = far[np.random.randint(len(far))]
    return np.exp2(a.ravel()).repeat(32)


def f64(x):
    return np.asarray(x).astype(np.float64)


def striped(idx):
    return np.tile(idx.reshape(-1, 16).T, (8, 1)).astype(np.uint16)


def unstriped(offs):
    return offs[:16].T.reshape(-1).astype(np.int64)


E2M1 = np.array([0.0, 0.5, 1.0, 1.5, 2.0, 3.0, 4.0, 6.0, -0.0, -0.5, -1.0, -1.5, -2.0, -3.0, -4.0, -6.0])


def pack_weight(w, fmt):
    k, n = w.shape
    w = f64(np.asarray(w, np.float32).astype(ml_dtypes.bfloat16)).reshape(k // 32, 32, n)
    amax = np.abs(w).max(1)
    if fmt == "e4m3":
        byte = np.frexp(amax)[1] - 1 + 127 - 7
    else:
        mant, ex = np.frexp(amax / 6.0)
        byte = np.where(mant > 0.5, ex, ex - 1) + 127
    byte = np.clip(np.where(amax > 0, byte, 1), 1, 254)
    scaled = (w * np.exp2(127.0 - byte)[:, None, :]).reshape(k, n).astype(np.float32)
    by_word = np.ascontiguousarray(scaled.reshape(k // 512, 128, 4, n).transpose(0, 1, 3, 2))
    if fmt == "e4m3":
        words = by_word.astype(ml_dtypes.float8_e4m3fn).view(np.uint8)
    else:
        c = by_word.astype(ml_dtypes.float4_e2m1fn).view(np.uint8) & 0xF
        words = (c[..., 0::2] | (c[..., 1::2] << 4)).reshape(k // 512, 128, 2 * n)
    return np.ascontiguousarray(words), np.ascontiguousarray(byte.astype(np.uint8).reshape(k // 512, 16, n))


def unpack_weight(words, scales, fmt):
    g, _, n = scales.shape
    words = np.ascontiguousarray(words).reshape(g, 128, n, -1)
    if fmt == "e4m3":
        vals = words.view(ml_dtypes.float8_e4m3fn).astype(np.float64)
    else:
        nib = np.empty((g, 128, n, 4), np.uint8)
        nib[..., 0::2] = words & 0xF
        nib[..., 1::2] = words >> 4
        vals = E2M1[nib]
    vals = vals * np.repeat(np.exp2(scales.astype(np.float64) - 127.0), 8, axis=1)[..., None]
    return vals.transpose(0, 1, 3, 2).reshape(g * 512, n)


def pack_table(v):
    words, scales = pack_weight(v, "e4m3")
    return np.concatenate([words.reshape(words.shape[0], -1), scales.reshape(scales.shape[0], -1)], axis=1)


def unpack_table(tab):
    g, t = tab.shape[0], tab.shape[1] // 528
    return unpack_weight(tab[:, :512 * t].reshape(g, 128, t, 4), tab[:, 512 * t:].reshape(g, 16, t), "e4m3")


def split(x):
    m, e = np.frexp(f64(x))
    hi = np.ldexp(np.trunc(16.0 * m) / 16.0, e)
    return hi, f64(x) - hi


def silu(v):
    return v / (1.0 + np.exp(-np.maximum(v, -700.0)))


K, M, T, S = 2048, 512, 4096, 2048


def setup_inputs():
    n = np.random.standard_normal
    s = mx_kscale(K)[:, None]
    return {
        "tab": pack_table(n((K, T)) * s),
        "w": (n((K, M)) / np.sqrt(K) / s).astype(np.float32),
        "b": (0.3 * n(512)).astype(np.float32),
        "offs": striped(np.random.permutation(T)[:S]),
    }


def reference(tab, w, b, offs):
    tab_ = unpack_table(tab)[:, unstriped(offs)]
    w_hi, w_lo = split(w)
    w_hi_, w_lo_ = mxq(w_hi, 0, "e4m3"), mxq(w_lo, 0, "e4m3")
    y = w_hi_.T @ tab_ + w_lo_.T @ tab_
    return silu(y + f64(b)[:, None])

@@ -1,0 +1,188 @@
+from contextlib import ExitStack
+
+import concourse.mybir as mybir
+
+K, M, T, S = 2048, 512, 4096, 2048
+FLOPS = 2 * 2 * K * M * S
+
+F32 = mybir.dt.float32
+BF16 = mybir.dt.bfloat16
+I32 = mybir.dt.int32
+U32 = mybir.dt.uint32
+U16 = mybir.dt.uint16
+U8 = mybir.dt.uint8
+FP8X4 = mybir.dt.float8_e4m3fn_x4
+
+P = 128
+PACK = 4
+K_PASS = P * PACK
+PASSES = K // K_PASS
+HALF = M // 2
+N_TILE = 512
+N_TILES = S // N_TILE
+HI_MASK = -983056
+
+
+def tile_list_tabw_hl_silu_kernel(tc, tab, w, b, offs, out):
+    nc = tc.nc
+    silu = mybir.ActivationFunctionType.Silu
+    band = mybir.AluOpType.bitwise_and
+    sub = mybir.AluOpType.subtract
+
+    with ExitStack() as ctx:
+        keep = ctx.enter_context(tc.tile_pool(name="keep", bufs=1))
+        stage = ctx.enter_context(tc.tile_pool(name="stage", bufs=4))
+        outs = ctx.enter_context(tc.tile_pool(name="outs", bufs=8))
+        psum = ctx.enter_context(tc.psum_pool(name="psum", bufs=8))
+
+        offsets = keep.tile([P, S // 16], U16, name="offsets")
+        nc.sync.dma_start(offsets[:], offs)
+
+        planes = keep.tile([P, T // 4], I32, name="planes", align_bytes=64)
+        nc.vector.memset(planes[:], 0)
+        bias = keep.tile([P, M // P], F32, name="bias")
+        with nc.allow_non_contiguous_dma(reason="512 bias values, one to a partition"):
+            nc.scalar.dma_start(out=bias[:], in_=b.rearrange("(m p) -> p m", p=P))
+        warm = keep.tile([P, 1], F32, name="warm")
+        nc.gpsimd.memset(warm[:], 0.0)
+        warm_out = keep.tile([P, 1], F32, name="warm_out")
+        nc.scalar.activation(out=warm_out[:], in_=warm[:], func=silu)
+
+        raws = {}
+
+        def load_w(half, a):
+            raw = keep.tile([P, PACK, HALF], F32, name="raw_%d_%d" % (half, a), align_bytes=64)
+            nc.sync.dma_start(
+                out=raw[:],
+                in_=w[a * K_PASS : (a + 1) * K_PASS, half * HALF : (half + 1) * HALF].rearrange("(p j) n -> p j n", j=PACK),
+            )
+            raws[(half, a)] = raw
+
+        words = []
+
+        def load_table(a):
+            t = keep.tile([P, T], I32, name="words%d" % a, align_bytes=64)
+            nc.sync.dma_start(out=t[:], in_=tab[a, 0 : K_PASS * T].rearrange("(p n) -> p n", p=P).bitcast(I32))
+            words.append(t)
+
+        for q in range(4):
+            rows = tab[:, K_PASS * T + 4 * q * T : K_PASS * T + 4 * (q + 1) * T].rearrange("a (r t) -> a r t", r=4).bitcast(I32)
+            nc.sync.dma_start(out=planes[32 * q : 32 * q + 16, :], in_=rows)
+        for a in range(PASSES):
+            load_w(0, a)
+        for a in range(PASSES):
+            load_table(a)
+        for a in range(PASSES):
+            load_w(1, a)
+
+        his = {}
+        los = {}
+        codes = {}
+
+        def split(half, a):
+            raw = raws[(half, a)]
+            top = stage.tile([P, HALF * PACK], BF16, name="top", align_bytes=64)
+            pairs = raw[:].rearrange("p j n -> p (j n)").bitcast(BF16).rearrange("p (j n e) -> p n j e", j=PACK, e=2)
+            nc.scalar.copy(out=top[:].rearrange("p (n j) -> p n j", j=PACK), in_=pairs[:, :, :, 1])
+            hi = stage.tile([P, HALF * PACK], BF16, name="hi", align_bytes=64)
+            nc.vector.tensor_scalar(out=hi[:].bitcast(I32), in0=top[:].bitcast(I32), scalar1=HI_MASK, scalar2=None, op0=band)
+            lo = stage.tile([P, HALF * PACK], BF16, name="lo", align_bytes=64)
+            (nc.vector if a % 2 == 0 else nc.gpsimd).tensor_tensor(
+                out=lo[:].rearrange("p (n j) -> p n j", j=PACK),
+                in0=raw[:].rearrange("p j n -> p n j"),
+                in1=hi[:].rearrange("p (n j) -> p n j", j=PACK),
+                op=sub,
+            )
+            his[(half, a)] = hi
+            los[(half, a)] = lo
+
+        def quantize(half, a, part):
+            source = (his if part == 0 else los)[(half, a)]
+            code = keep.tile([P, HALF], U32, name="code_%d_%d_%d" % (half, a, part), align_bytes=64)
+            scale = keep.tile([P, HALF], U8, name="scale_%d_%d_%d" % (half, a, part), align_bytes=64)
+            nc.vector.quantize_mx(out=code[:].bitcast(FP8X4), scales=scale[:], in_=source[:])
+            codes[(half, a, part)] = (code, scale)
+
+        picked_planes = keep.tile([P, S], U8, name="picked_planes", align_bytes=64)
+
+        def gather_planes(first, count):
+            nc.vector.tensor_copy(
+                out=picked_planes[:, first : first + count],
+                in_=planes[:].bitcast(U8).indirect(offsets[:, first // 16 : (first + count) // 16]),
+            )
+
+        picked = {}
+
+        def gather_words(a, first, count):
+            g = keep.tile([P, count], U32, name="picked_%d_%d" % (a, first), align_bytes=64)
+            nc.vector.tensor_copy(
+                out=g[:],
+                in_=words[a][:].bitcast(U32).indirect(offsets[:, first // 16 : (first + count) // 16]),
+            )
+            for n in range(first // N_TILE, (first + count) // N_TILE):
+                picked[(a, n)] = g[:, n * N_TILE - first : (n + 1) * N_TILE - first]
+
+        banks = {}
+
+        def multiply(m, n, a, part):
+            if a == 0 and part == 0:
+                banks[(m, n)] = psum.tile([P, N_TILE], F32, name="acc")
+            code, scale = codes[(m // 2, a, part)]
+            cols = slice((m % 2) * P, (m % 2 + 1) * P)
+            nc.tensor.matmul_mx(
+                out=banks[(m, n)][:],
+                lhsT=code[:, cols].bitcast(FP8X4),
+                lhsT_scale=scale[:, cols],
+                rhs=picked[(a, n)].bitcast(FP8X4),
+                rhs_scale=picked_planes[4 * a : P, n * N_TILE : (n + 1) * N_TILE],
+                start=(a == 0 and part == 0),
+                stop=(a == PASSES - 1 and part == 1),
+            )
+
+        def finish(m, n):
+            o = outs.tile([P, N_TILE], F32, name="o")
+            nc.scalar.activation(out=o[:], in_=banks[(m, n)][:], func=silu, bias=bias[:, m : m + 1])
+            nc.sync.dma_start(out=out[m * P : (m + 1) * P, n * N_TILE : (n + 1) * N_TILE], in_=o[:])
+
+        for a in range(PASSES):
+            split(0, a)
+            quantize(0, a, 0)
+            gather_planes(a * N_TILE, N_TILE)
+            quantize(0, a, 1)
+        for a in range(PASSES - 1):
+            gather_words(a, 0, S // 2)
+            gather_words(a, S // 2, S // 2)
+            for n in range(N_TILES):
+                for part in range(2):
+                    for m in range(2):
+                        multiply(m, n, a, part)
+        last = PASSES - 1
+        for n in range(N_TILES):
+            gather_words(last, n * N_TILE, N_TILE)
+            for part in range(2):
+                for m in range(2):
+                    multiply(m, n, last, part)
+            for m in range(2):
+                finish(m, n)
+            if n > 0:
+                split(1, n - 1)
+            if n > 1:
+                quantize(1, n - 2, 0)
+        quantize(1, 0, 1)
+        split(1, 3)
+        quantize(1, 1, 1)
+        quantize(1, 2, 0)
+        quantize(1, 2, 1)
+        quantize(1, 3, 0)
+        quantize(1, 3, 1)
+        for a in range(2):
+            for part in range(2):
+                for m in (2, 3):
+                    for n in range(N_TILES):
+                        multiply(m, n, a, part)
+        for m in (2, 3):
+            for n in range(N_TILES):
+                for a in (2, 3):
+                    for part in range(2):
+                        multiply(m, n, a, part)
+                finish(m, n)

@@ -32,6 +32,7 @@ def tile_list_tabw_hl_silu_kernel(tc, tab, w, b, offs, out):
     with ExitStack() as ctx:
         keep = ctx.enter_context(tc.tile_pool(name="keep", bufs=1))
         stage = ctx.enter_context(tc.tile_pool(name="stage", bufs=4))
+        big = ctx.enter_context(tc.tile_pool(name="big", bufs=4))
         outs = ctx.enter_context(tc.tile_pool(name="outs", bufs=8))
         psum = ctx.enter_context(tc.psum_pool(name="psum", bufs=8))
 
@@ -50,10 +51,9 @@ def tile_list_tabw_hl_silu_kernel(tc, tab, w, b, offs, out):
 
         raws = {}
 
-        def load_w(half, a):
-            raw = keep.tile([P, PACK, HALF], F32, name="raw_%d_%d" % (half, a), align_bytes=64)
+        def load_w(half, a, raw):
             nc.sync.dma_start(
-                out=raw[:],
+                out=raw,
                 in_=w[a * K_PASS : (a + 1) * K_PASS, half * HALF : (half + 1) * HALF].rearrange("(p j) n -> p j n", j=PACK),
             )
             raws[(half, a)] = raw
@@ -61,7 +61,7 @@ def tile_list_tabw_hl_silu_kernel(tc, tab, w, b, offs, out):
         words = []
 
         def load_table(a):
-            t = keep.tile([P, T], I32, name="words%d" % a, align_bytes=64)
+            t = big.tile([P, T], I32, name="words%d" % a, tag="big", align_bytes=64)
             nc.sync.dma_start(out=t[:], in_=tab[a, 0 : K_PASS * T].rearrange("(p n) -> p n", p=P).bitcast(I32))
             words.append(t)
 
@@ -69,31 +69,44 @@ def tile_list_tabw_hl_silu_kernel(tc, tab, w, b, offs, out):
             rows = tab[:, K_PASS * T + 4 * q * T : K_PASS * T + 4 * (q + 1) * T].rearrange("a (r t) -> a r t", r=4).bitcast(I32)
             nc.sync.dma_start(out=planes[32 * q : 32 * q + 16, :], in_=rows)
         for a in range(PASSES):
-            load_w(0, a)
+            raw = keep.tile([P, PACK, HALF], F32, name="raw%d" % a, align_bytes=64)
+            load_w(0, a, raw[:])
         for a in range(PASSES):
             load_table(a)
-        for a in range(PASSES):
-            load_w(1, a)
 
+        def load_second_half():
+            raw = big.tile([P, PASSES, PACK, HALF], F32, name="raw_second", tag="big", align_bytes=64)
+            for a in range(PASSES):
+                load_w(1, a, raw[:, a])
+
+        tops = {}
         his = {}
         los = {}
         codes = {}
 
-        def split(half, a):
+        def interleave(half, a):
             raw = raws[(half, a)]
             top = stage.tile([P, HALF * PACK], BF16, name="top", align_bytes=64)
-            pairs = raw[:].rearrange("p j n -> p (j n)").bitcast(BF16).rearrange("p (j n e) -> p n j e", j=PACK, e=2)
+            pairs = raw.rearrange("p j n -> p (j n)").bitcast(BF16).rearrange("p (j n e) -> p n j e", j=PACK, e=2)
             nc.scalar.copy(out=top[:].rearrange("p (n j) -> p n j", j=PACK), in_=pairs[:, :, :, 1])
+            tops[(half, a)] = top
+
+        def mask(half, a):
+            top = tops[(half, a)]
             hi = stage.tile([P, HALF * PACK], BF16, name="hi", align_bytes=64)
             nc.vector.tensor_scalar(out=hi[:].bitcast(I32), in0=top[:].bitcast(I32), scalar1=HI_MASK, scalar2=None, op0=band)
+            his[(half, a)] = hi
+
+        def subtract(half, a, engine):
+            raw = raws[(half, a)]
+            hi = his[(half, a)]
             lo = stage.tile([P, HALF * PACK], BF16, name="lo", align_bytes=64)
-            (nc.vector if a % 2 == 0 else nc.gpsimd).tensor_tensor(
+            engine.tensor_tensor(
                 out=lo[:].rearrange("p (n j) -> p n j", j=PACK),
-                in0=raw[:].rearrange("p j n -> p n j"),
+                in0=raw.rearrange("p j n -> p n j"),
                 in1=hi[:].rearrange("p (n j) -> p n j", j=PACK),
                 op=sub,
             )
-            his[(half, a)] = hi
             los[(half, a)] = lo
 
         def quantize(half, a, part):
@@ -145,13 +158,32 @@ def tile_list_tabw_hl_silu_kernel(tc, tab, w, b, offs, out):
             nc.sync.dma_start(out=out[m * P : (m + 1) * P, n * N_TILE : (n + 1) * N_TILE], in_=o[:])
 
         for a in range(PASSES):
-            split(0, a)
-            quantize(0, a, 0)
-            gather_planes(a * N_TILE, N_TILE)
-            quantize(0, a, 1)
+            interleave(0, a)
+        mask(0, 0)
+        mask(0, 1)
+        subtract(0, 1, nc.gpsimd)
+        gather_planes(0, N_TILE)
+        subtract(0, 0, nc.vector)
+        quantize(0, 0, 0)
+        mask(0, 2)
+        subtract(0, 2, nc.gpsimd)
+        gather_planes(N_TILE, N_TILE)
+        quantize(0, 0, 1)
+        mask(0, 3)
+        subtract(0, 3, nc.gpsimd)
+        gather_planes(2 * N_TILE, N_TILE)
+        quantize(0, 1, 0)
+        quantize(0, 1, 1)
+        gather_planes(3 * N_TILE, N_TILE)
+        quantize(0, 2, 0)
+        quantize(0, 2, 1)
+        quantize(0, 3, 0)
+        quantize(0, 3, 1)
         for a in range(PASSES - 1):
             gather_words(a, 0, S // 2)
             gather_words(a, S // 2, S // 2)
+            if a == 0:
+                load_second_half()
             for n in range(N_TILES):
                 for part in range(2):
                     for m in range(2):
@@ -164,12 +196,15 @@ def tile_list_tabw_hl_silu_kernel(tc, tab, w, b, offs, out):
                     multiply(m, n, last, part)
             for m in range(2):
                 finish(m, n)
+            interleave(1, n)
             if n > 0:
-                split(1, n - 1)
+                mask(1, n - 1)
+                subtract(1, n - 1, nc.gpsimd)
             if n > 1:
                 quantize(1, n - 2, 0)
         quantize(1, 0, 1)
-        split(1, 3)
+        mask(1, 3)
+        subtract(1, 3, nc.vector)
         quantize(1, 1, 1)
         quantize(1, 2, 0)
         quantize(1, 2, 1)

@@ -20,6 +20,7 @@ PASSES = K // K_PASS
 HALF = M // 2
 N_TILE = 512
 N_TILES = S // N_TILE
+SPLIT = 3072
 HI_MASK = -983056
 
 
@@ -32,7 +33,6 @@ def tile_list_tabw_hl_silu_kernel(tc, tab, w, b, offs, out):
     with ExitStack() as ctx:
         keep = ctx.enter_context(tc.tile_pool(name="keep", bufs=1))
         stage = ctx.enter_context(tc.tile_pool(name="stage", bufs=4))
-        big = ctx.enter_context(tc.tile_pool(name="big", bufs=4))
         outs = ctx.enter_context(tc.tile_pool(name="outs", bufs=8))
         psum = ctx.enter_context(tc.psum_pool(name="psum", bufs=8))
 
@@ -58,26 +58,24 @@ def tile_list_tabw_hl_silu_kernel(tc, tab, w, b, offs, out):
             )
             raws[(half, a)] = raw
 
-        words = []
+        words = [keep.tile([P, T], I32, name="words%d" % a, align_bytes=64) for a in range(PASSES)]
 
-        def load_table(a):
-            t = big.tile([P, T], I32, name="words%d" % a, tag="big", align_bytes=64)
-            nc.sync.dma_start(out=t[:], in_=tab[a, 0 : K_PASS * T].rearrange("(p n) -> p n", p=P).bitcast(I32))
-            words.append(t)
+        def load_table(a, cols):
+            rows = tab[a, 0 : K_PASS * T].rearrange("(p n) -> p n", p=P).bitcast(I32)
+            nc.sync.dma_start(out=words[a][:, cols], in_=rows[:, cols])
 
         for q in range(4):
             rows = tab[:, K_PASS * T + 4 * q * T : K_PASS * T + 4 * (q + 1) * T].rearrange("a (r t) -> a r t", r=4).bitcast(I32)
             nc.sync.dma_start(out=planes[32 * q : 32 * q + 16, :], in_=rows)
+        raw_tiles = [[keep.tile([P, PACK, HALF], F32, name="raw_%d_%d" % (h, a), align_bytes=64) for a in range(PASSES)] for h in range(2)]
+        load_w(0, 0, raw_tiles[0][0][:])
         for a in range(PASSES):
-            raw = keep.tile([P, PACK, HALF], F32, name="raw%d" % a, align_bytes=64)
-            load_w(0, a, raw[:])
+            load_table(a, slice(0, SPLIT))
+            if a < PASSES - 1:
+                load_w(0, a + 1, raw_tiles[0][a + 1][:])
+            load_table(a, slice(SPLIT, T))
         for a in range(PASSES):
-            load_table(a)
-
-        def load_second_half():
-            raw = big.tile([P, PASSES, PACK, HALF], F32, name="raw_second", tag="big", align_bytes=64)
-            for a in range(PASSES):
-                load_w(1, a, raw[:, a])
+            load_w(1, a, raw_tiles[1][a][:])
 
         tops = {}
         his = {}
@@ -157,33 +155,21 @@ def tile_list_tabw_hl_silu_kernel(tc, tab, w, b, offs, out):
             nc.scalar.activation(out=o[:], in_=banks[(m, n)][:], func=silu, bias=bias[:, m : m + 1])
             nc.sync.dma_start(out=out[m * P : (m + 1) * P, n * N_TILE : (n + 1) * N_TILE], in_=o[:])
 
-        for a in range(PASSES):
-            interleave(0, a)
+        interleave(0, 0)
         mask(0, 0)
-        mask(0, 1)
-        subtract(0, 1, nc.gpsimd)
-        gather_planes(0, N_TILE)
         subtract(0, 0, nc.vector)
         quantize(0, 0, 0)
-        mask(0, 2)
-        subtract(0, 2, nc.gpsimd)
-        gather_planes(N_TILE, N_TILE)
+        for n in range(N_TILES):
+            gather_planes(n * N_TILE, N_TILE)
         quantize(0, 0, 1)
-        mask(0, 3)
-        subtract(0, 3, nc.gpsimd)
-        gather_planes(2 * N_TILE, N_TILE)
-        quantize(0, 1, 0)
-        quantize(0, 1, 1)
-        gather_planes(3 * N_TILE, N_TILE)
-        quantize(0, 2, 0)
-        quantize(0, 2, 1)
-        quantize(0, 3, 0)
-        quantize(0, 3, 1)
         for a in range(PASSES - 1):
+            interleave(0, a + 1)
+            mask(0, a + 1)
+            subtract(0, a + 1, nc.gpsimd)
             gather_words(a, 0, S // 2)
             gather_words(a, S // 2, S // 2)
-            if a == 0:
-                load_second_half()
+            quantize(0, a + 1, 0)
+            quantize(0, a + 1, 1)
             for n in range(N_TILES):
                 for part in range(2):
                     for m in range(2):
@@ -199,7 +185,7 @@ def tile_list_tabw_hl_silu_kernel(tc, tab, w, b, offs, out):
             interleave(1, n)
             if n > 0:
                 mask(1, n - 1)
-                subtract(1, n - 1, nc.gpsimd)
+                subtract(1, n - 1, nc.vector)
             if n > 1:
                 quantize(1, n - 2, 0)
         quantize(1, 0, 1)

@@ -20,15 +20,15 @@ PASSES = K // K_PASS
 HALF = M // 2
 N_TILE = 512
 N_TILES = S // N_TILE
-SPLIT = 3072
+SPLIT = 2560
 HI_MASK = -983056
 
 
 def tile_list_tabw_hl_silu_kernel(tc, tab, w, b, offs, out):
     nc = tc.nc
     silu = mybir.ActivationFunctionType.Silu
-    band = mybir.AluOpType.bitwise_and
-    sub = mybir.AluOpType.subtract
+    bitwise_and = mybir.AluOpType.bitwise_and
+    subtract = mybir.AluOpType.subtract
 
     with ExitStack() as ctx:
         keep = ctx.enter_context(tc.tile_pool(name="keep", bufs=1))
@@ -46,106 +46,84 @@ def tile_list_tabw_hl_silu_kernel(tc, tab, w, b, offs, out):
             nc.scalar.dma_start(out=bias[:], in_=b.rearrange("(m p) -> p m", p=P))
         warm = keep.tile([P, 1], F32, name="warm")
         nc.gpsimd.memset(warm[:], 0.0)
-        warm_out = keep.tile([P, 1], F32, name="warm_out")
-        nc.scalar.activation(out=warm_out[:], in_=warm[:], func=silu)
-
-        raws = {}
-
-        def load_w(half, a, raw):
-            nc.sync.dma_start(
-                out=raw,
-                in_=w[a * K_PASS : (a + 1) * K_PASS, half * HALF : (half + 1) * HALF].rearrange("(p j) n -> p j n", j=PACK),
-            )
-            raws[(half, a)] = raw
+        nc.scalar.activation(out=warm[:], in_=warm[:], func=silu)
 
         words = [keep.tile([P, T], I32, name="words%d" % a, align_bytes=64) for a in range(PASSES)]
+        raws = {}
+        for half in range(2):
+            for a in range(PASSES):
+                raws[(half, a)] = keep.tile([P, PACK, HALF], F32, name="raw_%d_%d" % (half, a), align_bytes=64)
 
-        def load_table(a, cols):
+        def load_weights(half, a):
+            rows = w[a * K_PASS : (a + 1) * K_PASS, half * HALF : (half + 1) * HALF]
+            nc.sync.dma_start(out=raws[(half, a)][:], in_=rows.rearrange("(p j) n -> p j n", j=PACK))
+
+        def load_words(a, cols):
             rows = tab[a, 0 : K_PASS * T].rearrange("(p n) -> p n", p=P).bitcast(I32)
             nc.sync.dma_start(out=words[a][:, cols], in_=rows[:, cols])
 
         for q in range(4):
-            rows = tab[:, K_PASS * T + 4 * q * T : K_PASS * T + 4 * (q + 1) * T].rearrange("a (r t) -> a r t", r=4).bitcast(I32)
+            first = K_PASS * T + 4 * q * T
+            rows = tab[:, first : first + 4 * T].rearrange("a (r t) -> a r t", r=4).bitcast(I32)
             nc.sync.dma_start(out=planes[32 * q : 32 * q + 16, :], in_=rows)
-        raw_tiles = [[keep.tile([P, PACK, HALF], F32, name="raw_%d_%d" % (h, a), align_bytes=64) for a in range(PASSES)] for h in range(2)]
-        load_w(0, 0, raw_tiles[0][0][:])
+        load_weights(0, 0)
+        for a in range(PASSES - 1):
+            load_words(a, slice(0, SPLIT))
+            load_weights(0, a + 1)
+            load_words(a, slice(SPLIT, T))
+        load_words(PASSES - 1, slice(0, T))
         for a in range(PASSES):
-            load_table(a, slice(0, SPLIT))
-            if a < PASSES - 1:
-                load_w(0, a + 1, raw_tiles[0][a + 1][:])
-            load_table(a, slice(SPLIT, T))
-        for a in range(PASSES):
-            load_w(1, a, raw_tiles[1][a][:])
+            load_weights(1, a)
 
-        tops = {}
-        his = {}
-        los = {}
+        by_four = "p (c i j) -> p c j i"
+        parts = {}
         codes = {}
 
-        def interleave(half, a):
+        def split(half, a, engine):
             raw = raws[(half, a)]
             top = stage.tile([P, HALF * PACK], BF16, name="top", align_bytes=64)
-            pairs = raw.rearrange("p j n -> p (j n)").bitcast(BF16).rearrange("p (j n e) -> p n j e", j=PACK, e=2)
-            nc.scalar.copy(out=top[:].rearrange("p (n j) -> p n j", j=PACK), in_=pairs[:, :, :, 1])
-            tops[(half, a)] = top
-
-        def mask(half, a):
-            top = tops[(half, a)]
-            hi = stage.tile([P, HALF * PACK], BF16, name="hi", align_bytes=64)
-            nc.vector.tensor_scalar(out=hi[:].bitcast(I32), in0=top[:].bitcast(I32), scalar1=HI_MASK, scalar2=None, op0=band)
-            his[(half, a)] = hi
-
-        def subtract(half, a, engine):
-            raw = raws[(half, a)]
-            hi = his[(half, a)]
-            lo = stage.tile([P, HALF * PACK], BF16, name="lo", align_bytes=64)
+            halves = raw[:].rearrange("p j n -> p (j n)").bitcast(BF16).rearrange("p (j c i e) -> p c j i e", j=PACK, i=4, e=2)
+            nc.scalar.copy(out=top[:].rearrange(by_four, j=PACK, i=4), in_=halves[:, :, :, :, 1])
+            part = stage.tile([P, 2, HALF * PACK], BF16, name="part", align_bytes=64)
+            nc.vector.tensor_scalar(out=part[:, 0].bitcast(I32), in0=top[:].bitcast(I32), scalar1=HI_MASK, scalar2=None, op0=bitwise_and)
             engine.tensor_tensor(
-                out=lo[:].rearrange("p (n j) -> p n j", j=PACK),
-                in0=raw.rearrange("p j n -> p n j"),
-                in1=hi[:].rearrange("p (n j) -> p n j", j=PACK),
-                op=sub,
+                out=part[:, 1].rearrange(by_four, j=PACK, i=4),
+                in0=raw[:].rearrange("p j (c i) -> p c j i", i=4),
+                in1=part[:, 0].rearrange(by_four, j=PACK, i=4),
+                op=subtract,
             )
-            los[(half, a)] = lo
+            parts[(half, a)] = part
 
-        def quantize(half, a, part):
-            source = (his if part == 0 else los)[(half, a)]
-            code = keep.tile([P, HALF], U32, name="code_%d_%d_%d" % (half, a, part), align_bytes=64)
-            scale = keep.tile([P, HALF], U8, name="scale_%d_%d_%d" % (half, a, part), align_bytes=64)
-            nc.vector.quantize_mx(out=code[:].bitcast(FP8X4), scales=scale[:], in_=source[:])
-            codes[(half, a, part)] = (code, scale)
+        def quantize(half, a):
+            code = keep.tile([P, 2 * HALF], U32, name="code_%d_%d" % (half, a), align_bytes=64)
+            scale = keep.tile([P, 2 * HALF], U8, name="scale_%d_%d" % (half, a), align_bytes=64)
+            nc.vector.quantize_mx(out=code[:].bitcast(FP8X4), scales=scale[:], in_=parts[(half, a)][:].rearrange("p s e -> p (s e)"))
+            codes[(half, a)] = (code, scale)
 
         picked_planes = keep.tile([P, S], U8, name="picked_planes", align_bytes=64)
-
-        def gather_planes(first, count):
-            nc.vector.tensor_copy(
-                out=picked_planes[:, first : first + count],
-                in_=planes[:].bitcast(U8).indirect(offsets[:, first // 16 : (first + count) // 16]),
-            )
-
-        picked = {}
+        picked = [keep.tile([P, S], U32, name="picked%d" % a, align_bytes=64) for a in range(PASSES)]
 
         def gather_words(a, first, count):
-            g = keep.tile([P, count], U32, name="picked_%d_%d" % (a, first), align_bytes=64)
             nc.vector.tensor_copy(
-                out=g[:],
+                out=picked[a][:, first : first + count],
                 in_=words[a][:].bitcast(U32).indirect(offsets[:, first // 16 : (first + count) // 16]),
             )
-            for n in range(first // N_TILE, (first + count) // N_TILE):
-                picked[(a, n)] = g[:, n * N_TILE - first : (n + 1) * N_TILE - first]
 
         banks = {}
 
         def multiply(m, n, a, part):
             if a == 0 and part == 0:
                 banks[(m, n)] = psum.tile([P, N_TILE], F32, name="acc")
-            code, scale = codes[(m // 2, a, part)]
-            cols = slice((m % 2) * P, (m % 2 + 1) * P)
+            code, scale = codes[(m // 2, a)]
+            first = part * HALF + (m % 2) * P
+            cols = slice(first, first + P)
+            places = slice(n * N_TILE, (n + 1) * N_TILE)
             nc.tensor.matmul_mx(
                 out=banks[(m, n)][:],
                 lhsT=code[:, cols].bitcast(FP8X4),
                 lhsT_scale=scale[:, cols],
-                rhs=picked[(a, n)].bitcast(FP8X4),
-                rhs_scale=picked_planes[4 * a : P, n * N_TILE : (n + 1) * N_TILE],
+                rhs=picked[a][:, places].bitcast(FP8X4),
+                rhs_scale=picked_planes[4 * a : P, places],
                 start=(a == 0 and part == 0),
                 stop=(a == PASSES - 1 and part == 1),
             )
@@ -155,47 +133,31 @@ def tile_list_tabw_hl_silu_kernel(tc, tab, w, b, offs, out):
             nc.scalar.activation(out=o[:], in_=banks[(m, n)][:], func=silu, bias=bias[:, m : m + 1])
             nc.sync.dma_start(out=out[m * P : (m + 1) * P, n * N_TILE : (n + 1) * N_TILE], in_=o[:])
 
-        interleave(0, 0)
-        mask(0, 0)
-        subtract(0, 0, nc.vector)
-        quantize(0, 0, 0)
-        for n in range(N_TILES):
-            gather_planes(n * N_TILE, N_TILE)
-        quantize(0, 0, 1)
+        split(0, 0, nc.vector)
+        nc.vector.tensor_copy(out=picked_planes[:], in_=planes[:].bitcast(U8).indirect(offsets[:]))
+        quantize(0, 0)
         for a in range(PASSES - 1):
-            interleave(0, a + 1)
-            mask(0, a + 1)
-            subtract(0, a + 1, nc.gpsimd)
+            split(0, a + 1, nc.gpsimd)
             gather_words(a, 0, S // 2)
             gather_words(a, S // 2, S // 2)
-            quantize(0, a + 1, 0)
-            quantize(0, a + 1, 1)
+            quantize(0, a + 1)
             for n in range(N_TILES):
                 for part in range(2):
                     for m in range(2):
                         multiply(m, n, a, part)
-        last = PASSES - 1
         for n in range(N_TILES):
-            gather_words(last, n * N_TILE, N_TILE)
+            gather_words(PASSES - 1, n * N_TILE, N_TILE)
             for part in range(2):
                 for m in range(2):
-                    multiply(m, n, last, part)
+                    multiply(m, n, PASSES - 1, part)
             for m in range(2):
                 finish(m, n)
-            interleave(1, n)
-            if n > 0:
-                mask(1, n - 1)
-                subtract(1, n - 1, nc.vector)
-            if n > 1:
-                quantize(1, n - 2, 0)
-        quantize(1, 0, 1)
-        mask(1, 3)
-        subtract(1, 3, nc.vector)
-        quantize(1, 1, 1)
-        quantize(1, 2, 0)
-        quantize(1, 2, 1)
-        quantize(1, 3, 0)
-        quantize(1, 3, 1)
+            if n == 1:
+                split(1, 0, nc.vector)
+        quantize(1, 0)
+        for a in range(1, PASSES):
+            split(1, a, nc.vector)
+            quantize(1, a)
         for a in range(2):
             for part in range(2):
                 for m in (2, 3):

@@ -17,11 +17,20 @@ P = 128
 PACK = 4
 K_PASS = P * PACK
 PASSES = K // K_PASS
-HALF = M // 2
+M_TILE = 128
+M_TILES_HALF = 2
+HALF = M_TILES_HALF * M_TILE
 N_TILE = 512
 N_TILES = S // N_TILE
+BANKS = 8
+LIST_ROWS = 16
+ALIGN = 64
+
+HI_MASK = 0xFFF0FFF0 - 2**32
+
 SPLIT = 2560
-HI_MASK = -983056
+
+RUN = 4
 
 
 def tile_list_tabw_hl_silu_kernel(tc, tab, w, b, offs, out):
@@ -32,109 +41,137 @@ def tile_list_tabw_hl_silu_kernel(tc, tab, w, b, offs, out):
 
     with ExitStack() as ctx:
         keep = ctx.enter_context(tc.tile_pool(name="keep", bufs=1))
-        stage = ctx.enter_context(tc.tile_pool(name="stage", bufs=4))
-        outs = ctx.enter_context(tc.tile_pool(name="outs", bufs=8))
-        psum = ctx.enter_context(tc.psum_pool(name="psum", bufs=8))
+        stage = ctx.enter_context(tc.tile_pool(name="stage", bufs=PASSES))
+        outs = ctx.enter_context(tc.tile_pool(name="outs", bufs=BANKS))
+        psum = ctx.enter_context(tc.psum_pool(name="psum", bufs=BANKS))
 
-        offsets = keep.tile([P, S // 16], U16, name="offsets")
+        offsets = keep.tile([P, S // LIST_ROWS], U16, name="offsets")
         nc.sync.dma_start(offsets[:], offs)
 
-        planes = keep.tile([P, T // 4], I32, name="planes", align_bytes=64)
+        planes = keep.tile([P, T // 4], I32, name="planes", align_bytes=ALIGN)
         nc.vector.memset(planes[:], 0)
-        bias = keep.tile([P, M // P], F32, name="bias")
-        with nc.allow_non_contiguous_dma(reason="512 bias values, one to a partition"):
-            nc.scalar.dma_start(out=bias[:], in_=b.rearrange("(m p) -> p m", p=P))
+
         warm = keep.tile([P, 1], F32, name="warm")
         nc.gpsimd.memset(warm[:], 0.0)
         nc.scalar.activation(out=warm[:], in_=warm[:], func=silu)
 
-        words = [keep.tile([P, T], I32, name="words%d" % a, align_bytes=64) for a in range(PASSES)]
+        words = [keep.tile([P, T], I32, name="words%d" % a, align_bytes=ALIGN) for a in range(PASSES)]
         raws = {}
         for half in range(2):
             for a in range(PASSES):
-                raws[(half, a)] = keep.tile([P, PACK, HALF], F32, name="raw_%d_%d" % (half, a), align_bytes=64)
+                raws[(half, a)] = keep.tile([P, PACK, HALF], F32, name="raw_%d_%d" % (half, a), align_bytes=ALIGN)
+        bias = keep.tile([P, M // M_TILE], F32, name="bias")
 
         def load_weights(half, a):
             rows = w[a * K_PASS : (a + 1) * K_PASS, half * HALF : (half + 1) * HALF]
             nc.sync.dma_start(out=raws[(half, a)][:], in_=rows.rearrange("(p j) n -> p j n", j=PACK))
 
         def load_words(a, cols):
-            rows = tab[a, 0 : K_PASS * T].rearrange("(p n) -> p n", p=P).bitcast(I32)
+            rows = tab[a, 0 : K_PASS * T].rearrange("(p t) -> p t", p=P).bitcast(I32)
             nc.sync.dma_start(out=words[a][:, cols], in_=rows[:, cols])
 
-        for q in range(4):
-            first = K_PASS * T + 4 * q * T
-            rows = tab[:, first : first + 4 * T].rearrange("a (r t) -> a r t", r=4).bitcast(I32)
-            nc.sync.dma_start(out=planes[32 * q : 32 * q + 16, :], in_=rows)
         load_weights(0, 0)
-        for a in range(PASSES - 1):
-            load_words(a, slice(0, SPLIT))
-            load_weights(0, a + 1)
-            load_words(a, slice(SPLIT, T))
-        load_words(PASSES - 1, slice(0, T))
+
+        for quadrant in range(4):
+            first = K_PASS * T + 4 * quadrant * T
+            rows = tab[:, first : first + 4 * T].rearrange("a (r t) -> a r t", r=4).bitcast(I32)
+            nc.sync.dma_start(out=planes[32 * quadrant : 32 * quadrant + 16, :], in_=rows)
+
         for a in range(PASSES):
+            load_words(a, slice(0, SPLIT))
+            if a < PASSES - 1:
+                load_weights(0, a + 1)
+            else:
+                load_weights(1, 0)
+            load_words(a, slice(SPLIT, T))
+            if a == PASSES - 2:
+                with nc.allow_non_contiguous_dma(reason="512 bias values, one to a partition"):
+                    nc.sync.dma_start(out=bias[:], in_=b.rearrange("(m p) -> p m", p=P))
+        for a in range(1, PASSES):
             load_weights(1, a)
 
-        by_four = "p (c i j) -> p c j i"
+        interleaved = "p (c i j) -> p c j i"
         parts = {}
         codes = {}
 
         def split(half, a, engine):
             raw = raws[(half, a)]
-            top = stage.tile([P, HALF * PACK], BF16, name="top", align_bytes=64)
-            halves = raw[:].rearrange("p j n -> p (j n)").bitcast(BF16).rearrange("p (j c i e) -> p c j i e", j=PACK, i=4, e=2)
-            nc.scalar.copy(out=top[:].rearrange(by_four, j=PACK, i=4), in_=halves[:, :, :, :, 1])
-            part = stage.tile([P, 2, HALF * PACK], BF16, name="part", align_bytes=64)
-            nc.vector.tensor_scalar(out=part[:, 0].bitcast(I32), in0=top[:].bitcast(I32), scalar1=HI_MASK, scalar2=None, op0=bitwise_and)
+            upper = stage.tile([P, HALF * PACK], BF16, name="upper", align_bytes=ALIGN)
+            sixteens = raw[:].rearrange("p j n -> p (j n)").bitcast(BF16)
+            sixteens = sixteens.rearrange("p (j c i e) -> p c j i e", j=PACK, i=RUN, e=2)
+            nc.scalar.copy(out=upper[:].rearrange(interleaved, j=PACK, i=RUN), in_=sixteens[:, :, :, :, 1])
+            part = stage.tile([P, 2, HALF * PACK], BF16, name="part", align_bytes=ALIGN)
+            nc.vector.tensor_scalar(
+                out=part[:, 0].bitcast(I32),
+                in0=upper[:].bitcast(I32),
+                scalar1=HI_MASK,
+                scalar2=None,
+                op0=bitwise_and,
+            )
             engine.tensor_tensor(
-                out=part[:, 1].rearrange(by_four, j=PACK, i=4),
-                in0=raw[:].rearrange("p j (c i) -> p c j i", i=4),
-                in1=part[:, 0].rearrange(by_four, j=PACK, i=4),
+                out=part[:, 1].rearrange(interleaved, j=PACK, i=RUN),
+                in0=raw[:].rearrange("p j (c i) -> p c j i", i=RUN),
+                in1=part[:, 0].rearrange(interleaved, j=PACK, i=RUN),
                 op=subtract,
             )
             parts[(half, a)] = part
 
         def quantize(half, a):
-            code = keep.tile([P, 2 * HALF], U32, name="code_%d_%d" % (half, a), align_bytes=64)
-            scale = keep.tile([P, 2 * HALF], U8, name="scale_%d_%d" % (half, a), align_bytes=64)
-            nc.vector.quantize_mx(out=code[:].bitcast(FP8X4), scales=scale[:], in_=parts[(half, a)][:].rearrange("p s e -> p (s e)"))
+            code = keep.tile([P, 2 * HALF], U32, name="code_%d_%d" % (half, a), align_bytes=ALIGN)
+            scale = keep.tile([P, 2 * HALF], U8, name="scale_%d_%d" % (half, a), align_bytes=ALIGN)
+            nc.vector.quantize_mx(
+                out=code[:].bitcast(FP8X4),
+                scales=scale[:],
+                in_=parts[(half, a)][:].rearrange("p s e -> p (s e)"),
+            )
             codes[(half, a)] = (code, scale)
 
-        picked_planes = keep.tile([P, S], U8, name="picked_planes", align_bytes=64)
-        picked = [keep.tile([P, S], U32, name="picked%d" % a, align_bytes=64) for a in range(PASSES)]
+        picked_planes = keep.tile([P, S], U8, name="picked_planes", align_bytes=ALIGN)
+        picked = [keep.tile([P, S], U32, name="picked%d" % a, align_bytes=ALIGN) for a in range(PASSES)]
+
+        def list_part(first, count):
+            return offsets[:, first // LIST_ROWS : (first + count) // LIST_ROWS]
+
+        def gather_scales(first, count):
+            nc.vector.tensor_copy(
+                out=picked_planes[:, first : first + count],
+                in_=planes[:].bitcast(U8).indirect(list_part(first, count)),
+            )
 
         def gather_words(a, first, count):
             nc.vector.tensor_copy(
                 out=picked[a][:, first : first + count],
-                in_=words[a][:].bitcast(U32).indirect(offsets[:, first // 16 : (first + count) // 16]),
+                in_=words[a][:].bitcast(U32).indirect(list_part(first, count)),
             )
 
-        banks = {}
+        sums = {}
 
-        def multiply(m, n, a, part):
-            if a == 0 and part == 0:
-                banks[(m, n)] = psum.tile([P, N_TILE], F32, name="acc")
-            code, scale = codes[(m // 2, a)]
-            first = part * HALF + (m % 2) * P
-            cols = slice(first, first + P)
-            places = slice(n * N_TILE, (n + 1) * N_TILE)
+        def multiply(m, n, a, part, left=0, width=N_TILE):
+            if (m, n) not in sums:
+                sums[(m, n)] = psum.tile([M_TILE, N_TILE], F32, name="acc")
+            code, scale = codes[(m // M_TILES_HALF, a)]
+            first = part * HALF + (m % M_TILES_HALF) * M_TILE
+            channels = slice(first, first + M_TILE)
+            places = slice(n * N_TILE + left, n * N_TILE + left + width)
             nc.tensor.matmul_mx(
-                out=banks[(m, n)][:],
-                lhsT=code[:, cols].bitcast(FP8X4),
-                lhsT_scale=scale[:, cols],
+                out=sums[(m, n)][:, left : left + width],
+                lhsT=code[:, channels].bitcast(FP8X4),
+                lhsT_scale=scale[:, channels],
                 rhs=picked[a][:, places].bitcast(FP8X4),
                 rhs_scale=picked_planes[4 * a : P, places],
                 start=(a == 0 and part == 0),
                 stop=(a == PASSES - 1 and part == 1),
             )
 
-        def finish(m, n):
-            o = outs.tile([P, N_TILE], F32, name="o")
-            nc.scalar.activation(out=o[:], in_=banks[(m, n)][:], func=silu, bias=bias[:, m : m + 1])
-            nc.sync.dma_start(out=out[m * P : (m + 1) * P, n * N_TILE : (n + 1) * N_TILE], in_=o[:])
+        def finish(m, n, left=0, width=N_TILE):
+            done = outs.tile([M_TILE, width], F32, name="done")
+            nc.scalar.activation(out=done[:], in_=sums[(m, n)][:, left : left + width], func=silu, bias=bias[:, m : m + 1])
+            rows = slice(m * M_TILE, (m + 1) * M_TILE)
+            nc.sync.dma_start(out=out[rows, n * N_TILE + left : n * N_TILE + left + width], in_=done[:])
 
-        split(0, 0, nc.vector)
-        nc.vector.tensor_copy(out=picked_planes[:], in_=planes[:].bitcast(U8).indirect(offsets[:]))
+        split(0, 0, nc.gpsimd)
+        for n in range(N_TILES):
+            gather_scales(n * N_TILE, N_TILE)
         quantize(0, 0)
         for a in range(PASSES - 1):
             split(0, a + 1, nc.gpsimd)
@@ -143,29 +180,35 @@ def tile_list_tabw_hl_silu_kernel(tc, tab, w, b, offs, out):
             quantize(0, a + 1)
             for n in range(N_TILES):
                 for part in range(2):
-                    for m in range(2):
+                    for m in range(M_TILES_HALF):
                         multiply(m, n, a, part)
+        split(1, 0, nc.gpsimd)
         for n in range(N_TILES):
             gather_words(PASSES - 1, n * N_TILE, N_TILE)
             for part in range(2):
-                for m in range(2):
+                for m in range(M_TILES_HALF):
                     multiply(m, n, PASSES - 1, part)
-            for m in range(2):
+            for m in range(M_TILES_HALF):
                 finish(m, n)
-            if n == 1:
-                split(1, 0, nc.vector)
+
         quantize(1, 0)
         for a in range(1, PASSES):
             split(1, a, nc.vector)
             quantize(1, a)
-        for a in range(2):
+        banks = [(m, n) for m in range(M_TILES_HALF, 2 * M_TILES_HALF) for n in range(N_TILES)]
+        second, last = banks[:-1], banks[-1]
+        early = PASSES // 2
+        for a in range(early):
             for part in range(2):
-                for m in (2, 3):
-                    for n in range(N_TILES):
-                        multiply(m, n, a, part)
-        for m in (2, 3):
-            for n in range(N_TILES):
-                for a in (2, 3):
-                    for part in range(2):
-                        multiply(m, n, a, part)
-                finish(m, n)
+                for m, n in second:
+                    multiply(m, n, a, part)
+        for m, n in second:
+            for a in range(early, PASSES):
+                for part in range(2):
+                    multiply(m, n, a, part)
+            finish(m, n)
+        for left in range(0, N_TILE, N_TILE // 2):
+            for a in range(PASSES):
+                for part in range(2):
+                    multiply(*last, a, part, left, N_TILE // 2)
+            finish(*last, left, N_TILE // 2)

from contextlib import ExitStack

import concourse.mybir as mybir

K, M, T, S = 2048, 512, 4096, 2048
FLOPS = 2 * 2 * K * M * S

F32 = mybir.dt.float32
BF16 = mybir.dt.bfloat16
I32 = mybir.dt.int32
U32 = mybir.dt.uint32
U16 = mybir.dt.uint16
U8 = mybir.dt.uint8
FP8X4 = mybir.dt.float8_e4m3fn_x4

P = 128
PACK = 4
K_PASS = P * PACK
PASSES = K // K_PASS
M_TILE = 128
M_TILES_HALF = 2
HALF = M_TILES_HALF * M_TILE
N_TILE = 512
N_TILES = S // N_TILE
BANKS = 8
LIST_ROWS = 16
ALIGN = 64

HI_MASK = 0xFFF0FFF0 - 2**32

SPLIT = 2560

RUN = 4


def tile_list_tabw_hl_silu_kernel(tc, tab, w, b, offs, out):
    nc = tc.nc
    silu = mybir.ActivationFunctionType.Silu
    bitwise_and = mybir.AluOpType.bitwise_and
    subtract = mybir.AluOpType.subtract

    with ExitStack() as ctx:
        keep = ctx.enter_context(tc.tile_pool(name="keep", bufs=1))
        stage = ctx.enter_context(tc.tile_pool(name="stage", bufs=PASSES))
        outs = ctx.enter_context(tc.tile_pool(name="outs", bufs=BANKS))
        psum = ctx.enter_context(tc.psum_pool(name="psum", bufs=BANKS))

        offsets = keep.tile([P, S // LIST_ROWS], U16, name="offsets")
        nc.sync.dma_start(offsets[:], offs)

        planes = keep.tile([P, T // 4], I32, name="planes", align_bytes=ALIGN)
        nc.vector.memset(planes[:], 0)

        warm = keep.tile([P, 1], F32, name="warm")
        nc.gpsimd.memset(warm[:], 0.0)
        nc.scalar.activation(out=warm[:], in_=warm[:], func=silu)

        words = [keep.tile([P, T], I32, name="words%d" % a, align_bytes=ALIGN) for a in range(PASSES)]
        raws = {}
        for half in range(2):
            for a in range(PASSES):
                raws[(half, a)] = keep.tile([P, PACK, HALF], F32, name="raw_%d_%d" % (half, a), align_bytes=ALIGN)
        bias = keep.tile([P, M // M_TILE], F32, name="bias")

        def load_weights(half, a):
            rows = w[a * K_PASS : (a + 1) * K_PASS, half * HALF : (half + 1) * HALF]
            nc.sync.dma_start(out=raws[(half, a)][:], in_=rows.rearrange("(p j) n -> p j n", j=PACK))

        def load_words(a, cols):
            rows = tab[a, 0 : K_PASS * T].rearrange("(p t) -> p t", p=P).bitcast(I32)
            nc.sync.dma_start(out=words[a][:, cols], in_=rows[:, cols])

        load_weights(0, 0)

        for quadrant in range(4):
            first = K_PASS * T + 4 * quadrant * T
            rows = tab[:, first : first + 4 * T].rearrange("a (r t) -> a r t", r=4).bitcast(I32)
            nc.sync.dma_start(out=planes[32 * quadrant : 32 * quadrant + 16, :], in_=rows)

        for a in range(PASSES):
            load_words(a, slice(0, SPLIT))
            if a < PASSES - 1:
                load_weights(0, a + 1)
            else:
                load_weights(1, 0)
            load_words(a, slice(SPLIT, T))
            if a == PASSES - 2:
                with nc.allow_non_contiguous_dma(reason="512 bias values, one to a partition"):
                    nc.sync.dma_start(out=bias[:], in_=b.rearrange("(m p) -> p m", p=P))
        for a in range(1, PASSES):
            load_weights(1, a)

        interleaved = "p (c i j) -> p c j i"
        parts = {}
        codes = {}

        def split(half, a, engine):
            raw = raws[(half, a)]
            upper = stage.tile([P, HALF * PACK], BF16, name="upper", align_bytes=ALIGN)
            sixteens = raw[:].rearrange("p j n -> p (j n)").bitcast(BF16)
            sixteens = sixteens.rearrange("p (j c i e) -> p c j i e", j=PACK, i=RUN, e=2)
            nc.scalar.copy(out=upper[:].rearrange(interleaved, j=PACK, i=RUN), in_=sixteens[:, :, :, :, 1])
            part = stage.tile([P, 2, HALF * PACK], BF16, name="part", align_bytes=ALIGN)
            nc.vector.tensor_scalar(
                out=part[:, 0].bitcast(I32),
                in0=upper[:].bitcast(I32),
                scalar1=HI_MASK,
                scalar2=None,
                op0=bitwise_and,
            )
            engine.tensor_tensor(
                out=part[:, 1].rearrange(interleaved, j=PACK, i=RUN),
                in0=raw[:].rearrange("p j (c i) -> p c j i", i=RUN),
                in1=part[:, 0].rearrange(interleaved, j=PACK, i=RUN),
                op=subtract,
            )
            parts[(half, a)] = part

        def quantize(half, a):
            code = keep.tile([P, 2 * HALF], U32, name="code_%d_%d" % (half, a), align_bytes=ALIGN)
            scale = keep.tile([P, 2 * HALF], U8, name="scale_%d_%d" % (half, a), align_bytes=ALIGN)
            nc.vector.quantize_mx(
                out=code[:].bitcast(FP8X4),
                scales=scale[:],
                in_=parts[(half, a)][:].rearrange("p s e -> p (s e)"),
            )
            codes[(half, a)] = (code, scale)

        picked_planes = keep.tile([P, S], U8, name="picked_planes", align_bytes=ALIGN)
        picked = [keep.tile([P, S], U32, name="picked%d" % a, align_bytes=ALIGN) for a in range(PASSES)]

        def list_part(first, count):
            return offsets[:, first // LIST_ROWS : (first + count) // LIST_ROWS]

        def gather_scales(first, count):
            nc.vector.tensor_copy(
                out=picked_planes[:, first : first + count],
                in_=planes[:].bitcast(U8).indirect(list_part(first, count)),
            )

        def gather_words(a, first, count):
            nc.vector.tensor_copy(
                out=picked[a][:, first : first + count],
                in_=words[a][:].bitcast(U32).indirect(list_part(first, count)),
            )

        sums = {}

        def multiply(m, n, a, part, left=0, width=N_TILE):
            if (m, n) not in sums:
                sums[(m, n)] = psum.tile([M_TILE, N_TILE], F32, name="acc")
            code, scale = codes[(m // M_TILES_HALF, a)]
            first = part * HALF + (m % M_TILES_HALF) * M_TILE
            channels = slice(first, first + M_TILE)
            places = slice(n * N_TILE + left, n * N_TILE + left + width)
            nc.tensor.matmul_mx(
                out=sums[(m, n)][:, left : left + width],
                lhsT=code[:, channels].bitcast(FP8X4),
                lhsT_scale=scale[:, channels],
                rhs=picked[a][:, places].bitcast(FP8X4),
                rhs_scale=picked_planes[4 * a : P, places],
                start=(a == 0 and part == 0),
                stop=(a == PASSES - 1 and part == 1),
            )

        def finish(m, n, left=0, width=N_TILE):
            done = outs.tile([M_TILE, width], F32, name="done")
            nc.scalar.activation(out=done[:], in_=sums[(m, n)][:, left : left + width], func=silu, bias=bias[:, m : m + 1])
            rows = slice(m * M_TILE, (m + 1) * M_TILE)
            nc.sync.dma_start(out=out[rows, n * N_TILE + left : n * N_TILE + left + width], in_=done[:])

        split(0, 0, nc.gpsimd)
        for n in range(N_TILES):
            gather_scales(n * N_TILE, N_TILE)
        quantize(0, 0)
        for a in range(PASSES - 1):
            split(0, a + 1, nc.gpsimd)
            gather_words(a, 0, S // 2)
            gather_words(a, S // 2, S // 2)
            quantize(0, a + 1)
            for n in range(N_TILES):
                for part in range(2):
                    for m in range(M_TILES_HALF):
                        multiply(m, n, a, part)
        split(1, 0, nc.gpsimd)
        for n in range(N_TILES):
            gather_words(PASSES - 1, n * N_TILE, N_TILE)
            for part in range(2):
                for m in range(M_TILES_HALF):
                    multiply(m, n, PASSES - 1, part)
            for m in range(M_TILES_HALF):
                finish(m, n)

        quantize(1, 0)
        for a in range(1, PASSES):
            split(1, a, nc.vector)
            quantize(1, a)
        banks = [(m, n) for m in range(M_TILES_HALF, 2 * M_TILES_HALF) for n in range(N_TILES)]
        second, last = banks[:-1], banks[-1]
        early = PASSES // 2
        for a in range(early):
            for part in range(2):
                for m, n in second:
                    multiply(m, n, a, part)
        for m, n in second:
            for a in range(early, PASSES):
                for part in range(2):
                    multiply(m, n, a, part)
            finish(m, n)
        for left in range(0, N_TILE, N_TILE // 2):
            for a in range(PASSES):
                for part in range(2):
                    multiply(*last, a, part, left, N_TILE // 2)
            finish(*last, left, N_TILE // 2)
